import numpy as np
import ml_dtypes


def mxq(x, axis, fmt="e4m3"):
    dtype, down = {"e4m3": (ml_dtypes.float8_e4m3fn, 7), "e5m2": (ml_dtypes.float8_e5m2, 14)}[fmt]
    v = np.moveaxis(np.asarray(x, np.float32).astype(ml_dtypes.bfloat16).astype(np.float64), axis, -1)
    blocks = v.reshape(v.shape[:-1] + (-1, 32))
    amax = np.abs(blocks).max(-1, keepdims=True)
    byte = np.maximum(np.where(amax > 0, np.frexp(amax)[1] - 1 + 127, 0) - down, 1)
    scale = np.exp2(byte - 127.0)
    codes = (blocks / scale).astype(np.float32).astype(dtype).astype(np.float64)
    return np.moveaxis((codes * scale).reshape(v.shape), -1, axis)


WIDE = False


def mx_kscale(k):
    if not WIDE:
        return np.ones(k)
    levels = np.array([10, -10, 5, -5, 0])
    if k % 512:
        return np.exp2(np.random.permutation(np.resize(levels, k // 32))).repeat(32)
    a = np.empty((k // 512, 16))
    for p in range(k // 512):
        a[p, :8] = np.random.permutation(np.resize(levels, 8))
        for g in range(8):
            far = levels[np.abs(levels - a[p, g]) >= 10]
            a[p, g + 8] = far[np.random.randint(len(far))]
    return np.exp2(a.ravel()).repeat(32)


def f64(x):
    return np.asarray(x).astype(np.float64)


def striped(idx):
    return np.tile(np.asarray(idx).reshape(-1, 16).T, (8, 1)).astype(np.uint16)


def unstriped(offs):
    return offs[:16].T.reshape(-1).astype(np.int64)


D, T, I, Q, E = 512, 1024, 512, 128, 512


def setup_inputs():
    n = np.random.standard_normal
    idx = np.random.permutation(T)[:I]
    idx2 = np.random.permutation(T)[:I]
    fd = mx_kscale(D)
    fi = mx_kscale(I)
    return {
        "query": (n((D, Q)) * 0.25 / np.sqrt(D) * fd[:, None]).astype(np.float32),
        "keys": (n((D, T)) / fd[:, None]).astype(np.float32),
        "size": (np.random.uniform(0.5, 2.0, (1, I)) * fi).astype(np.float32),
        "vals": (n((E, T))).astype(np.float32),
        "vsc": (np.random.uniform(0.3, 1.0, (I, 1)) / fi[:, None]).astype(np.float32),
        "offs": striped(idx),
        "offs2": striped(idx2),
    }


def reference(query, keys, size, vals, vsc, offs, offs2):
    idx = unstriped(offs)
    idx2 = unstriped(offs2)
    km = np.maximum(f64(keys)[:, idx], f64(keys)[:, idx2])
    queryq = mxq(f64(query), 0, "e4m3")
    kmq = mxq(km, 0, "e4m3")
    a = queryq.T @ kmq
    p = np.exp(a - np.max(a, axis=1, keepdims=True))
    w = p * f64(size) / np.sum(p, axis=1, keepdims=True)
    wt = w.T
    v1 = f64(vals)[:, idx].T
    v2 = f64(vals)[:, idx2].T
    vv = (v1 + v2) * f64(vsc)
    wtq = mxq(wt, 0, "e4m3")
    vvq = mxq(vv, 0, "e4m3")
    o = wtq.T @ vvq
    return o

@@ -1,0 +1,202 @@
+from contextlib import ExitStack
+
+import concourse.mybir as mybir
+from concourse.masks import make_identity
+
+D, T, I, Q, E = 512, 1024, 512, 128, 512
+FLOPS = 2 * D * Q * I + 2 * I * Q * E
+
+F32 = mybir.dt.float32
+BF16 = mybir.dt.bfloat16
+U32 = mybir.dt.uint32
+U16 = mybir.dt.uint16
+U8 = mybir.dt.uint8
+FP8X4 = mybir.dt.float8_e4m3fn_x4
+ALU = mybir.AluOpType
+ACT = mybir.ActivationFunctionType
+
+P = 128
+PACK = 4
+LINE = 4
+BLOCKS = E // P
+
+
+def tile_attend_maxmerge_kernel(tc, query, keys, size, vals, vsc, offs, offs2, out):
+    nc = tc.nc
+    with ExitStack() as ctx:
+        sb = ctx.enter_context(tc.tile_pool(name="sb", bufs=1))
+        ps = ctx.enter_context(tc.psum_pool(name="ps", bufs=1))
+
+        list1 = sb.tile([P, I // 16], U16, name="list1")
+        list2 = sb.tile([P, I // 16], U16, name="list2")
+        key_planes = [sb.tile([P, T], F32, name=f"key_plane{t}") for t in range(PACK)]
+        val_rows = [sb.tile([P, T], F32, name=f"val_rows{j}") for j in range(BLOCKS)]
+        q_raw = sb.tile([P, PACK, Q], F32, name="q_raw")
+        vsc_col = sb.tile([P, PACK], F32, name="vsc_col")
+        size_col = sb.tile([P, PACK], F32, name="size_col")
+
+        keys_by_place = keys.rearrange("(p t) n -> t p n", t=PACK)
+        nc.sync.dma_start(list1[:], offs)
+        nc.sync.dma_start(key_planes[0][:], keys_by_place[0])
+        nc.sync.dma_start(list2[:], offs2)
+        for t in range(1, PACK):
+            nc.sync.dma_start(key_planes[t][:], keys_by_place[t])
+        nc.sync.dma_start(q_raw[:], query.rearrange("(p t) q -> p t q", t=PACK))
+        for j in range(BLOCKS):
+            nc.sync.dma_start(val_rows[j][:], vals[j * P : (j + 1) * P, :])
+        nc.sync.dma_start(vsc_col[:], vsc.rearrange("(p t) o -> p (t o)", t=PACK))
+        nc.sync.dma_start(size_col[:], size.rearrange("o (p t) -> p (o t)", t=PACK))
+
+        ident = sb.tile([P, P], F32, name="ident")
+        make_identity(nc, ident[:])
+
+        def mx_tiles(name, width, tag):
+            codes = sb.tile([P, width], U32, name=f"{name}_codes", tag=tag, align_bytes=64)
+            scales = sb.tile([P, width], U8, name=f"{name}_scales", align_bytes=64)
+            return codes, scales
+
+        def quantize_into(mx, grouped, cols):
+            nc.vector.quantize_mx(
+                out=mx[0][:, cols].bitcast(FP8X4),
+                scales=mx[1][:, cols],
+                in_=grouped[:, cols, :].rearrange("p n t -> p (n t)"),
+            )
+
+        def quantize(name, grouped):
+            mx = mx_tiles(name, P, f"{name}_codes")
+            quantize_into(mx, grouped, slice(0, P))
+            return mx
+
+        def mx_product(acc, stationary, moving):
+            nc.tensor.matmul_mx(
+                out=acc,
+                lhsT=stationary[0][:].bitcast(FP8X4),
+                lhsT_scale=stationary[1][:],
+                rhs=moving[0][:].bitcast(FP8X4),
+                rhs_scale=moving[1][:],
+                start=True,
+                stop=True,
+            )
+
+        def by_place(planes):
+            return planes.rearrange("p t (c i) -> p c t i", i=LINE)
+
+        def woven(grouped):
+            return grouped.rearrange("p (c i) t -> p c t i", i=LINE)
+
+        def scale_planes(name, bank, factor):
+            planes = sb.tile([P, PACK, P], BF16, name=f"{name}_planes", tag=f"{name}_planes", align_bytes=64)
+            for t in range(PACK):
+                nc.scalar.activation(planes[:, t, :], bank[:, t, :], ACT.Copy, scale=factor[:, t : t + 1])
+            return planes
+
+        def weave(name, planes):
+            grouped = sb.tile([P, P, PACK], BF16, name=f"{name}_grouped", align_bytes=64)
+            nc.scalar.copy(woven(grouped[:]), by_place(planes[:]))
+            return grouped
+
+        def gather_vals(j, which, tag):
+            picked = sb.tile([P, PACK, P], F32, name=f"picked{j}_{which}", tag=tag, align_bytes=64)
+            nc.vector.tensor_copy(
+                picked[:].bitcast(U32).rearrange("p t s -> p s t"),
+                val_rows[j][:].bitcast(U32).indirect((list1, list2)[which][:]),
+            )
+            for t in range(PACK):
+                nc.tensor.matmul(
+                    banks[j][:, t, :],
+                    lhsT=picked[:, t, :],
+                    rhs=ident[:],
+                    start=(which == 0 and t == 0),
+                    stop=(which == 1 and t == PACK - 1),
+                    is_transpose=True,
+                )
+
+        def store(name, bank_tag, blocks, first, copy, queue):
+            width = len(blocks) * P
+            acc = ps.tile([Q, width], F32, name=f"{name}_acc", tag=bank_tag)
+            for n, vv_mx in enumerate(blocks):
+                mx_product(acc[:, n * P : (n + 1) * P], w_mx, vv_mx)
+            res = sb.tile([Q, width], F32, name=f"{name}_res")
+            copy(res[:], acc[:])
+            queue.dma_start(out[:, first * P : first * P + width], res[:])
+
+        q_grouped = sb.tile([P, Q, PACK], BF16, name="q_grouped", align_bytes=64)
+        nc.scalar.copy(woven(q_grouped[:]), by_place(q_raw[:]))
+        q_mx = quantize("q", q_grouped)
+
+        halves = [slice(0, I // 2), slice(I // 2, I)]
+        keys1 = sb.tile([P, PACK, I], F32, name="keys1")
+        keys2 = sb.tile([P, PACK, I], F32, name="keys2")
+        for t in range(PACK):
+            nc.vector.tensor_copy(keys1[:, t, :], key_planes[t][:].indirect(list1[:]))
+            if t < PACK - 1:
+                nc.vector.tensor_copy(keys2[:, t, :], key_planes[t][:].indirect(list2[:]))
+            else:
+                for h in halves:
+                    nc.vector.tensor_copy(
+                        keys2[:, t, h], key_planes[t][:].indirect(list2[:, h.start // 16 : h.stop // 16])
+                    )
+        km_grouped = sb.tile([P, I, PACK], BF16, name="km_grouped", align_bytes=64)
+        for h in halves:
+            nc.vector.tensor_tensor(
+                woven(km_grouped[:, h, :]), by_place(keys1[:, :, h]), by_place(keys2[:, :, h]), ALU.max
+            )
+        km_mx = mx_tiles("km", I, "km_codes")
+        for h in halves:
+            quantize_into(km_mx, km_grouped, h)
+        scores = ps.tile([Q, I], F32, name="scores", tag="scores")
+        mx_product(scores[:], q_mx, km_mx)
+
+        banks = [ps.tile([P, PACK, P], F32, name=f"val_bank{j}", tag=f"val_bank{j}") for j in range(BLOCKS)]
+        gather_vals(0, 0, "picked_first")
+
+        neg_max = sb.tile([Q, 1], F32, name="neg_max", tag="neg_max", align_bytes=64)
+        nc.vector.tensor_reduce(neg_max[:], scores[:], mybir.AxisListType.X, ALU.max, negate=True)
+        p_dealt = sb.tile([Q, PACK, P], F32, name="p_dealt", tag="p_dealt", align_bytes=64)
+        row_sum = sb.tile([Q, 1], F32, name="row_sum", tag="row_sum", align_bytes=64)
+        nc.scalar.activation(
+            p_dealt[:],
+            scores[:].rearrange("q (s t) -> q t s", t=PACK),
+            ACT.Exp,
+            bias=neg_max[:],
+            accum_out=row_sum[:],
+        )
+        gather_vals(0, 1, "km_codes")
+
+        inv_sum = sb.tile([Q, 1], F32, name="inv_sum")
+        nc.vector.reciprocal(inv_sum[:], row_sum[:])
+        p_normed = sb.tile([Q, PACK, P], F32, name="p_normed", tag="p_normed", align_bytes=64)
+        nc.scalar.activation(p_normed[:], p_dealt[:], ACT.Copy, scale=inv_sum[:])
+        w_bank = ps.tile([P, PACK, Q], F32, name="w_bank", tag="w_bank")
+        for t in range(PACK):
+            nc.tensor.transpose(w_bank[:, t, :], p_normed[:, t, :], ident[:])
+        gather_vals(1, 0, "neg_max")
+        vv_planes0 = scale_planes("vv0", banks[0], vsc_col)
+        w_planes = scale_planes("w", w_bank, size_col)
+        gather_vals(1, 1, "row_sum")
+        vv_grouped0 = weave("vv0", vv_planes0)
+        w_grouped = weave("w", w_planes)
+        gather_vals(2, 0, "p_dealt")
+        vv_mx0 = quantize("vv0", vv_grouped0)
+        vv_planes1 = scale_planes("vv1", banks[1], vsc_col)
+        vv_grouped1 = weave("vv1", vv_planes1)
+        gather_vals(2, 1, "p_normed")
+        w_mx = quantize("w", w_grouped)
+        gather_vals(3, 0, "vv0_planes")
+        vv_mx1 = quantize("vv1", vv_grouped1)
+        vv_planes2 = scale_planes("vv2", banks[2], vsc_col)
+        vv_grouped2 = weave("vv2", vv_planes2)
+        gather_vals(3, 1, "w_planes")
+        store("early", "scores", [vv_mx0, vv_mx1], 0, nc.scalar.copy, nc.sync)
+        vv_mx2 = quantize("vv2", vv_grouped2)
+        store("third", "w_bank", [vv_mx2], 2, nc.scalar.copy, nc.sync)
+
+        vv_grouped3 = sb.tile([P, P, PACK], BF16, name="vv3_grouped", align_bytes=64)
+        nc.vector.tensor_tensor(
+            vv_grouped3[:],
+            banks[3][:].rearrange("p t e -> p e t"),
+            vsc_col[:].unsqueeze(1).to_broadcast([P, P, PACK]),
+            ALU.mult,
+        )
+        vv_mx3 = quantize("vv3", vv_grouped3)
+        store("last", "last_acc", [vv_mx3], 3, nc.vector.tensor_copy, nc.sync)

@@ -18,6 +18,7 @@ ACT = mybir.ActivationFunctionType
 P = 128
 PACK = 4
 LINE = 4
+RUN = 8
 BLOCKS = E // P
 
 
@@ -32,23 +33,36 @@ def tile_attend_maxmerge_kernel(tc, query, keys, size, vals, vsc, offs, offs2, o
         key_planes = [sb.tile([P, T], F32, name=f"key_plane{t}") for t in range(PACK)]
         val_rows = [sb.tile([P, T], F32, name=f"val_rows{j}") for j in range(BLOCKS)]
         q_raw = sb.tile([P, PACK, Q], F32, name="q_raw")
-        vsc_col = sb.tile([P, PACK], F32, name="vsc_col")
-        size_col = sb.tile([P, PACK], F32, name="size_col")
+        factor_rows = sb.tile([P, P], F32, name="factor_rows")
+        nc.gpsimd.memset(factor_rows[:], 0.0)
 
         keys_by_place = keys.rearrange("(p t) n -> t p n", t=PACK)
         nc.sync.dma_start(list1[:], offs)
         nc.sync.dma_start(key_planes[0][:], keys_by_place[0])
         nc.sync.dma_start(list2[:], offs2)
-        for t in range(1, PACK):
+        nc.sync.dma_start(key_planes[1][:], keys_by_place[1])
+        nc.sync.dma_start(
+            factor_rows[0:PACK, :].rearrange("t (g j) -> t g j", j=RUN),
+            vsc.rearrange("(g t j) o -> t g (j o)", t=PACK, j=RUN),
+        )
+        nc.sync.dma_start(
+            factor_rows[PACK : 2 * PACK, :].rearrange("t (g j) -> t g j", j=RUN),
+            size.rearrange("o (g t j) -> t (o g) j", t=PACK, j=RUN),
+        )
+        for t in range(2, PACK):
             nc.sync.dma_start(key_planes[t][:], keys_by_place[t])
         nc.sync.dma_start(q_raw[:], query.rearrange("(p t) q -> p t q", t=PACK))
         for j in range(BLOCKS):
             nc.sync.dma_start(val_rows[j][:], vals[j * P : (j + 1) * P, :])
-        nc.sync.dma_start(vsc_col[:], vsc.rearrange("(p t) o -> p (t o)", t=PACK))
-        nc.sync.dma_start(size_col[:], size.rearrange("o (p t) -> p (o t)", t=PACK))
 
         ident = sb.tile([P, P], F32, name="ident")
         make_identity(nc, ident[:])
+        factor_bank = ps.tile([P, P], F32, name="factor_bank", tag="last_acc")
+        nc.tensor.transpose(factor_bank[:], factor_rows[:], ident[:])
+        factor_cols = sb.tile([P, 2 * PACK], F32, name="factor_cols")
+        nc.scalar.copy(factor_cols[:], factor_bank[:, 0 : 2 * PACK])
+        vsc_col = factor_cols[:, 0:PACK]
+        size_col = factor_cols[:, PACK : 2 * PACK]
 
         def mx_tiles(name, width, tag):
             codes = sb.tile([P, width], U32, name=f"{name}_codes", tag=tag, align_bytes=64)
@@ -91,14 +105,24 @@ def tile_attend_maxmerge_kernel(tc, query, keys, size, vals, vsc, offs, offs2, o
             return planes
 
         def weave(name, planes):
-            grouped = sb.tile([P, P, PACK], BF16, name=f"{name}_grouped", align_bytes=64)
+            grouped = sb.tile([P, P, PACK], BF16, name=f"{name}_grouped", tag=f"{name}_grouped", align_bytes=64)
             nc.scalar.copy(woven(grouped[:]), by_place(planes[:]))
+            return grouped
+
+        def scale_woven(name, bank, tag):
+            grouped = sb.tile([P, P, PACK], BF16, name=f"{name}_grouped", tag=tag, align_bytes=64)
+            nc.vector.tensor_tensor(
+                grouped[:],
+                bank[:].rearrange("p t e -> p e t"),
+                vsc_col.unsqueeze(1).to_broadcast([P, P, PACK]),
+                ALU.mult,
+            )
             return grouped
 
         def gather_vals(j, which, tag):
             picked = sb.tile([P, PACK, P], F32, name=f"picked{j}_{which}", tag=tag, align_bytes=64)
             nc.vector.tensor_copy(
-                picked[:].bitcast(U32).rearrange("p t s -> p s t"),
+                picked[:].bitcast(U32).rearrange("p t (g j) -> p g t j", j=RUN),
                 val_rows[j][:].bitcast(U32).indirect((list1, list2)[which][:]),
             )
             for t in range(PACK):
@@ -155,8 +179,8 @@ def tile_attend_maxmerge_kernel(tc, query, keys, size, vals, vsc, offs, offs2, o
         p_dealt = sb.tile([Q, PACK, P], F32, name="p_dealt", tag="p_dealt", align_bytes=64)
         row_sum = sb.tile([Q, 1], F32, name="row_sum", tag="row_sum", align_bytes=64)
         nc.scalar.activation(
-            p_dealt[:],
-            scores[:].rearrange("q (s t) -> q t s", t=PACK),
+            p_dealt[:].rearrange("q t (g j) -> q t g j", j=RUN),
+            scores[:].rearrange("q (g t j) -> q t g j", t=PACK, j=RUN),
             ACT.Exp,
             bias=neg_max[:],
             accum_out=row_sum[:],
@@ -177,26 +201,19 @@ def tile_attend_maxmerge_kernel(tc, query, keys, size, vals, vsc, offs, offs2, o
         vv_grouped0 = weave("vv0", vv_planes0)
         w_grouped = weave("w", w_planes)
         gather_vals(2, 0, "p_dealt")
-        vv_mx0 = quantize("vv0", vv_grouped0)
         vv_planes1 = scale_planes("vv1", banks[1], vsc_col)
         vv_grouped1 = weave("vv1", vv_planes1)
         gather_vals(2, 1, "p_normed")
-        w_mx = quantize("w", w_grouped)
-        gather_vals(3, 0, "vv0_planes")
-        vv_mx1 = quantize("vv1", vv_grouped1)
+        gather_vals(3, 0, "p_dealt")
+        gather_vals(3, 1, "p_normed")
         vv_planes2 = scale_planes("vv2", banks[2], vsc_col)
         vv_grouped2 = weave("vv2", vv_planes2)
-        gather_vals(3, 1, "w_planes")
-        store("early", "scores", [vv_mx0, vv_mx1], 0, nc.scalar.copy, nc.sync)
+        vv_mx0 = quantize("vv0", vv_grouped0)
+        w_mx = quantize("w", w_grouped)
+        vv_mx1 = quantize("vv1", vv_grouped1)
+        vv_grouped3 = scale_woven("vv3", banks[3], "vv2_planes")
         vv_mx2 = quantize("vv2", vv_grouped2)
-        store("third", "w_bank", [vv_mx2], 2, nc.scalar.copy, nc.sync)
-
-        vv_grouped3 = sb.tile([P, P, PACK], BF16, name="vv3_grouped", align_bytes=64)
-        nc.vector.tensor_tensor(
-            vv_grouped3[:],
-            banks[3][:].rearrange("p t e -> p e t"),
-            vsc_col[:].unsqueeze(1).to_broadcast([P, P, PACK]),
-            ALU.mult,
-        )
         vv_mx3 = quantize("vv3", vv_grouped3)
+        store("early", "val_bank2", [vv_mx0, vv_mx1], 0, nc.scalar.copy, nc.sync)
+        store("third", "w_bank", [vv_mx2], 2, nc.scalar.copy, nc.sync)
         store("last", "last_acc", [vv_mx3], 3, nc.vector.tensor_copy, nc.sync)

from contextlib import ExitStack

import concourse.mybir as mybir
from concourse.masks import make_identity

D, T, I, Q, E = 512, 1024, 512, 128, 512
FLOPS = 2 * D * Q * I + 2 * I * Q * E

F32 = mybir.dt.float32
BF16 = mybir.dt.bfloat16
U32 = mybir.dt.uint32
U16 = mybir.dt.uint16
U8 = mybir.dt.uint8
FP8X4 = mybir.dt.float8_e4m3fn_x4
ALU = mybir.AluOpType
ACT = mybir.ActivationFunctionType

P = 128
PACK = 4
LINE = 4
RUN = 8
BLOCKS = E // P


def tile_attend_maxmerge_kernel(tc, query, keys, size, vals, vsc, offs, offs2, out):
    nc = tc.nc
    with ExitStack() as ctx:
        sb = ctx.enter_context(tc.tile_pool(name="sb", bufs=1))
        ps = ctx.enter_context(tc.psum_pool(name="ps", bufs=1))

        list1 = sb.tile([P, I // 16], U16, name="list1")
        list2 = sb.tile([P, I // 16], U16, name="list2")
        key_planes = [sb.tile([P, T], F32, name=f"key_plane{t}") for t in range(PACK)]
        val_rows = [sb.tile([P, T], F32, name=f"val_rows{j}") for j in range(BLOCKS)]
        q_raw = sb.tile([P, PACK, Q], F32, name="q_raw")
        factor_rows = sb.tile([P, P], F32, name="factor_rows")
        nc.gpsimd.memset(factor_rows[:], 0.0)

        keys_by_place = keys.rearrange("(p t) n -> t p n", t=PACK)
        nc.sync.dma_start(list1[:], offs)
        nc.sync.dma_start(key_planes[0][:], keys_by_place[0])
        nc.sync.dma_start(list2[:], offs2)
        nc.sync.dma_start(key_planes[1][:], keys_by_place[1])
        nc.sync.dma_start(
            factor_rows[0:PACK, :].rearrange("t (g j) -> t g j", j=RUN),
            vsc.rearrange("(g t j) o -> t g (j o)", t=PACK, j=RUN),
        )
        nc.sync.dma_start(
            factor_rows[PACK : 2 * PACK, :].rearrange("t (g j) -> t g j", j=RUN),
            size.rearrange("o (g t j) -> t (o g) j", t=PACK, j=RUN),
        )
        for t in range(2, PACK):
            nc.sync.dma_start(key_planes[t][:], keys_by_place[t])
        nc.sync.dma_start(q_raw[:], query.rearrange("(p t) q -> p t q", t=PACK))
        for j in range(BLOCKS):
            nc.sync.dma_start(val_rows[j][:], vals[j * P : (j + 1) * P, :])

        ident = sb.tile([P, P], F32, name="ident")
        make_identity(nc, ident[:])
        factor_bank = ps.tile([P, P], F32, name="factor_bank", tag="last_acc")
        nc.tensor.transpose(factor_bank[:], factor_rows[:], ident[:])
        factor_cols = sb.tile([P, 2 * PACK], F32, name="factor_cols")
        nc.scalar.copy(factor_cols[:], factor_bank[:, 0 : 2 * PACK])
        vsc_col = factor_cols[:, 0:PACK]
        size_col = factor_cols[:, PACK : 2 * PACK]

        def mx_tiles(name, width, tag):
            codes = sb.tile([P, width], U32, name=f"{name}_codes", tag=tag, align_bytes=64)
            scales = sb.tile([P, width], U8, name=f"{name}_scales", align_bytes=64)
            return codes, scales

        def quantize_into(mx, grouped, cols):
            nc.vector.quantize_mx(
                out=mx[0][:, cols].bitcast(FP8X4),
                scales=mx[1][:, cols],
                in_=grouped[:, cols, :].rearrange("p n t -> p (n t)"),
            )

        def quantize(name, grouped):
            mx = mx_tiles(name, P, f"{name}_codes")
            quantize_into(mx, grouped, slice(0, P))
            return mx

        def mx_product(acc, stationary, moving):
            nc.tensor.matmul_mx(
                out=acc,
                lhsT=stationary[0][:].bitcast(FP8X4),
                lhsT_scale=stationary[1][:],
                rhs=moving[0][:].bitcast(FP8X4),
                rhs_scale=moving[1][:],
                start=True,
                stop=True,
            )

        def by_place(planes):
            return planes.rearrange("p t (c i) -> p c t i", i=LINE)

        def woven(grouped):
            return grouped.rearrange("p (c i) t -> p c t i", i=LINE)

        def scale_planes(name, bank, factor):
            planes = sb.tile([P, PACK, P], BF16, name=f"{name}_planes", tag=f"{name}_planes", align_bytes=64)
            for t in range(PACK):
                nc.scalar.activation(planes[:, t, :], bank[:, t, :], ACT.Copy, scale=factor[:, t : t + 1])
            return planes

        def weave(name, planes):
            grouped = sb.tile([P, P, PACK], BF16, name=f"{name}_grouped", tag=f"{name}_grouped", align_bytes=64)
            nc.scalar.copy(woven(grouped[:]), by_place(planes[:]))
            return grouped

        def scale_woven(name, bank, tag):
            grouped = sb.tile([P, P, PACK], BF16, name=f"{name}_grouped", tag=tag, align_bytes=64)
            nc.vector.tensor_tensor(
                grouped[:],
                bank[:].rearrange("p t e -> p e t"),
                vsc_col.unsqueeze(1).to_broadcast([P, P, PACK]),
                ALU.mult,
            )
            return grouped

        def gather_vals(j, which, tag):
            picked = sb.tile([P, PACK, P], F32, name=f"picked{j}_{which}", tag=tag, align_bytes=64)
            nc.vector.tensor_copy(
                picked[:].bitcast(U32).rearrange("p t (g j) -> p g t j", j=RUN),
                val_rows[j][:].bitcast(U32).indirect((list1, list2)[which][:]),
            )
            for t in range(PACK):
                nc.tensor.matmul(
                    banks[j][:, t, :],
                    lhsT=picked[:, t, :],
                    rhs=ident[:],
                    start=(which == 0 and t == 0),
                    stop=(which == 1 and t == PACK - 1),
                    is_transpose=True,
                )

        def store(name, bank_tag, blocks, first, copy, queue):
            width = len(blocks) * P
            acc = ps.tile([Q, width], F32, name=f"{name}_acc", tag=bank_tag)
            for n, vv_mx in enumerate(blocks):
                mx_product(acc[:, n * P : (n + 1) * P], w_mx, vv_mx)
            res = sb.tile([Q, width], F32, name=f"{name}_res")
            copy(res[:], acc[:])
            queue.dma_start(out[:, first * P : first * P + width], res[:])

        q_grouped = sb.tile([P, Q, PACK], BF16, name="q_grouped", align_bytes=64)
        nc.scalar.copy(woven(q_grouped[:]), by_place(q_raw[:]))
        q_mx = quantize("q", q_grouped)

        halves = [slice(0, I // 2), slice(I // 2, I)]
        keys1 = sb.tile([P, PACK, I], F32, name="keys1")
        keys2 = sb.tile([P, PACK, I], F32, name="keys2")
        for t in range(PACK):
            nc.vector.tensor_copy(keys1[:, t, :], key_planes[t][:].indirect(list1[:]))
            if t < PACK - 1:
                nc.vector.tensor_copy(keys2[:, t, :], key_planes[t][:].indirect(list2[:]))
            else:
                for h in halves:
                    nc.vector.tensor_copy(
                        keys2[:, t, h], key_planes[t][:].indirect(list2[:, h.start // 16 : h.stop // 16])
                    )
        km_grouped = sb.tile([P, I, PACK], BF16, name="km_grouped", align_bytes=64)
        for h in halves:
            nc.vector.tensor_tensor(
                woven(km_grouped[:, h, :]), by_place(keys1[:, :, h]), by_place(keys2[:, :, h]), ALU.max
            )
        km_mx = mx_tiles("km", I, "km_codes")
        for h in halves:
            quantize_into(km_mx, km_grouped, h)
        scores = ps.tile([Q, I], F32, name="scores", tag="scores")
        mx_product(scores[:], q_mx, km_mx)

        banks = [ps.tile([P, PACK, P], F32, name=f"val_bank{j}", tag=f"val_bank{j}") for j in range(BLOCKS)]
        gather_vals(0, 0, "picked_first")

        neg_max = sb.tile([Q, 1], F32, name="neg_max", tag="neg_max", align_bytes=64)
        nc.vector.tensor_reduce(neg_max[:], scores[:], mybir.AxisListType.X, ALU.max, negate=True)
        p_dealt = sb.tile([Q, PACK, P], F32, name="p_dealt", tag="p_dealt", align_bytes=64)
        row_sum = sb.tile([Q, 1], F32, name="row_sum", tag="row_sum", align_bytes=64)
        nc.scalar.activation(
            p_dealt[:].rearrange("q t (g j) -> q t g j", j=RUN),
            scores[:].rearrange("q (g t j) -> q t g j", t=PACK, j=RUN),
            ACT.Exp,
            bias=neg_max[:],
            accum_out=row_sum[:],
        )
        gather_vals(0, 1, "km_codes")

        inv_sum = sb.tile([Q, 1], F32, name="inv_sum")
        nc.vector.reciprocal(inv_sum[:], row_sum[:])
        p_normed = sb.tile([Q, PACK, P], F32, name="p_normed", tag="p_normed", align_bytes=64)
        nc.scalar.activation(p_normed[:], p_dealt[:], ACT.Copy, scale=inv_sum[:])
        w_bank = ps.tile([P, PACK, Q], F32, name="w_bank", tag="w_bank")
        for t in range(PACK):
            nc.tensor.transpose(w_bank[:, t, :], p_normed[:, t, :], ident[:])
        gather_vals(1, 0, "neg_max")
        vv_planes0 = scale_planes("vv0", banks[0], vsc_col)
        w_planes = scale_planes("w", w_bank, size_col)
        gather_vals(1, 1, "row_sum")
        vv_grouped0 = weave("vv0", vv_planes0)
        w_grouped = weave("w", w_planes)
        gather_vals(2, 0, "p_dealt")
        vv_planes1 = scale_planes("vv1", banks[1], vsc_col)
        vv_grouped1 = weave("vv1", vv_planes1)
        gather_vals(2, 1, "p_normed")
        gather_vals(3, 0, "p_dealt")
        gather_vals(3, 1, "p_normed")
        vv_planes2 = scale_planes("vv2", banks[2], vsc_col)
        vv_grouped2 = weave("vv2", vv_planes2)
        vv_mx0 = quantize("vv0", vv_grouped0)
        w_mx = quantize("w", w_grouped)
        vv_mx1 = quantize("vv1", vv_grouped1)
        vv_grouped3 = scale_woven("vv3", banks[3], "vv2_planes")
        vv_mx2 = quantize("vv2", vv_grouped2)
        vv_mx3 = quantize("vv3", vv_grouped3)
        store("early", "val_bank2", [vv_mx0, vv_mx1], 0, nc.scalar.copy, nc.sync)
        store("third", "w_bank", [vv_mx2], 2, nc.scalar.copy, nc.sync)
        store("last", "last_acc", [vv_mx3], 3, nc.vector.tensor_copy, nc.sync)
